import numpy as np
import ml_dtypes


def mxq(x, axis, fmt="e4m3"):
    dtype, down = {"e4m3": (ml_dtypes.float8_e4m3fn, 7), "e5m2": (ml_dtypes.float8_e5m2, 14)}[fmt]
    v = np.moveaxis(np.asarray(x, np.float32).astype(ml_dtypes.bfloat16).astype(np.float64), axis, -1)
    blocks = v.reshape(v.shape[:-1] + (-1, 32))
    amax = np.abs(blocks).max(-1, keepdims=True)
    byte = np.maximum(np.where(amax > 0, np.frexp(amax)[1] - 1 + 127, 0) - down, 1)
    scale = np.exp2(byte - 127.0)
    codes = (blocks / scale).astype(np.float32).astype(dtype).astype(np.float64)
    return np.moveaxis((codes * scale).reshape(v.shape), -1, axis)


WIDE = False


def mx_kscale(k):
    if not WIDE:
        return np.ones(k)
    levels = np.array([30, -30])
    if k % 512:
        return np.exp2(np.random.permutation(np.resize(levels, k // 32))).repeat(32)
    a = np.empty((k // 512, 16))
    for p in range(k // 512):
        a[p, :8] = np.random.permutation(np.resize(levels, 8))
        for g in range(8):
            far = levels[np.abs(levels - a[p, g]) >= 10]
            a[p, g + 8] = far[np.random.randint(len(far))]
    return np.exp2(a.ravel()).repeat(32)


def f64(x):
    return np.asarray(x).astype(np.float64)


def striped(idx):
    return np.tile(np.asarray(idx).reshape(-1, 16).T, (8, 1)).astype(np.uint16)


def unstriped(offs):
    return offs[:16].T.reshape(-1).astype(np.int64)


E2M1 = np.array([0.0, 0.5, 1.0, 1.5, 2.0, 3.0, 4.0, 6.0, -0.0, -0.5, -1.0, -1.5, -2.0, -3.0, -4.0, -6.0])


def pack_weight(w, fmt):
    k, n = w.shape
    w = f64(np.asarray(w, np.float32).astype(ml_dtypes.bfloat16)).reshape(k // 32, 32, n)
    amax = np.abs(w).max(1)
    if fmt in ("e4m3", "e5m2"):
        byte = np.frexp(amax)[1] - 1 + 127 - (7 if fmt == "e4m3" else 14)
    else:
        mant, ex = np.frexp(amax / 6.0)
        byte = np.where(mant > 0.5, ex, ex - 1) + 127
    byte = np.clip(np.where(amax > 0, byte, 1), 1, 254)
    scaled = (w * np.exp2(127.0 - byte)[:, None, :]).reshape(k, n).astype(np.float32)
    by_word = np.ascontiguousarray(scaled.reshape(k // 512, 128, 4, n).transpose(0, 1, 3, 2))
    if fmt in ("e4m3", "e5m2"):
        words = by_word.astype(ml_dtypes.float8_e4m3fn if fmt == "e4m3" else ml_dtypes.float8_e5m2).view(np.uint8)
    else:
        c = by_word.astype(ml_dtypes.float4_e2m1fn).view(np.uint8) & 0xF
        words = (c[..., 0::2] | (c[..., 1::2] << 4)).reshape(k // 512, 128, 2 * n)
    return np.ascontiguousarray(words), np.ascontiguousarray(byte.astype(np.uint8).reshape(k // 512, 16, n))


def unpack_weight(words, scales, fmt):
    g, _, n = scales.shape
    words = np.ascontiguousarray(words).reshape(g, 128, n, -1)
    if fmt in ("e4m3", "e5m2"):
        vals = words.view(ml_dtypes.float8_e4m3fn if fmt == "e4m3" else ml_dtypes.float8_e5m2).astype(np.float64)
    else:
        nib = np.empty((g, 128, n, 4), np.uint8)
        nib[..., 0::2] = words & 0xF
        nib[..., 1::2] = words >> 4
        vals = E2M1[nib]
    vals = vals * np.repeat(np.exp2(scales.astype(np.float64) - 127.0), 8, axis=1)[..., None]
    return vals.transpose(0, 1, 3, 2).reshape(g * 512, n)


K, T, J, R, C, O, N = 1024, 1024, 256, 512, 1024, 256, 256


def setup_inputs():
    n = np.random.standard_normal
    idx = np.random.permutation(T)[:J]
    idx2 = np.random.permutation(C)[:J]
    idx3 = np.random.permutation(C)[:O]
    fk = mx_kscale(K)
    fr = mx_kscale(R)
    wp = pack_weight(n((K, R)) * 1 / np.sqrt(K) * fk[:, None] * fr, "e5m2")
    wbp = pack_weight(n((R, N)) * 1 / np.sqrt(R) / fr[:, None], "e2m1")
    return {
        "xf": (n((K, T))).astype(np.float32),
        "ow": (n((K, J)) * 0.7).astype(np.float32),
        "fk": (np.random.uniform(0.5, 2.0, (K, 1)) / fk[:, None]).astype(np.float32),
        "w_words": wp[0],
        "w_scales": wp[1],
        "oldh": (n((R, C)) * 0.7 * fr[:, None]).astype(np.float32),
        "wb_words": wbp[0],
        "wb_scales": wbp[1],
        "bi": (np.random.uniform(-0.5, 0.5, (1, N))).astype(np.float32),
        "offs": striped(idx),
        "offs2": striped(idx2),
        "offs3": striped(idx3),
    }


def reference(xf, ow, fk, w_words, w_scales, oldh, wb_words, wb_scales, bi, offs, offs2, offs3):
    idx = unstriped(offs)
    idx2 = unstriped(offs2)
    idx3 = unstriped(offs3)
    wu = unpack_weight(w_words, w_scales, "e5m2")
    wbu = unpack_weight(wb_words, wb_scales, "e2m1")
    u = (f64(xf)[:, idx] - f64(ow)) * f64(fk)
    uq = mxq(u, 0, "e5m2")
    a = wu.T @ uq
    ha = np.maximum(a, 0.0)
    pw0 = np.zeros((R, C))
    pw0[:, idx2] = ha
    pg = pw0 + f64(oldh)
    hid = pg[:, idx3]
    hidq = mxq(hid, 0, "e5m2")
    p = hidq.T @ wbu
    ea = np.exp(0.7 * p + f64(bi))
    y = 256.0 * ea / np.sum(ea, axis=1, keepdims=True)
    return y

@@ -1,0 +1,146 @@
+from contextlib import ExitStack
+
+import concourse.mybir as mybir
+
+K, T, J, R, C, O, N = 1024, 1024, 256, 512, 1024, 256, 256
+FLOPS = 2 * K * R * J + 2 * R * O * N
+
+F32 = mybir.dt.float32
+BF16 = mybir.dt.bfloat16
+I32 = mybir.dt.int32
+U32 = mybir.dt.uint32
+U16 = mybir.dt.uint16
+U8 = mybir.dt.uint8
+E5M2 = mybir.dt.float8_e5m2_x4
+E2M1 = mybir.dt.float4_e2m1fn_x4
+ALU = mybir.AluOpType
+ACT = mybir.ActivationFunctionType
+AX = mybir.AxisListType
+
+P = 128
+PACK = 4
+PASSES = K // (P * PACK)
+HALF = O // 2
+
+
+def tile_list_page_offsetpicks_rowshares_kernel(tc, xf, ow, fk, w_words, w_scales, oldh, wb_words, wb_scales, bi, offs, offs2, offs3, out):
+    nc = tc.nc
+    with ExitStack() as ctx:
+        keep = ctx.enter_context(tc.tile_pool(name="keep", bufs=1))
+        psum = ctx.enter_context(tc.psum_pool(name="psum", bufs=1))
+
+        l1 = keep.tile([P, J // 16], U16, name="l1")
+        l2 = keep.tile([P, J // 16], U16, name="l2")
+        l3 = keep.tile([P, O // 16], U16, name="l3")
+        x = [[keep.tile([P, T], F32, name="x%d%d" % (z, t)) for t in range(PACK)] for z in range(PASSES)]
+        ctr = [keep.tile([P, PACK, J], F32, name="ctr%d" % z) for z in range(PASSES)]
+        fac = keep.tile([P, PASSES, PACK], F32, name="fac")
+        wraw = [keep.tile([P, R], U32, name="wraw%d" % z, align_bytes=64) for z in range(PASSES)]
+        wsraw = keep.tile([P, PASSES, R], U8, name="wsraw", align_bytes=64)
+        wd = [keep.tile([P, R], U32, name="wd%d" % z, align_bytes=64) for z in range(PASSES)]
+        wsd = keep.tile([P, PASSES, R], U8, name="wsd", align_bytes=64)
+        old = [keep.tile([P, C], F32, name="old%d" % t) for t in range(PACK)]
+        placed = [keep.tile([P, C], F32, name="placed%d" % t) for t in range(PACK)]
+        page = [keep.tile([P, C], F32, name="page%d" % t) for t in range(PACK)]
+        wb = keep.tile([P, 2 * N], U8, name="wb", align_bytes=64)
+        wbs = keep.tile([P, N], U8, name="wbs", align_bytes=64)
+        bias = keep.tile([P, N], F32, name="bias")
+
+        xv = xf.rearrange("(z p t) c -> z t p c", z=PASSES, t=PACK)
+        owv = ow.rearrange("(z p t) j -> z p t j", z=PASSES, t=PACK)
+        oldv = oldh.rearrange("(p t) c -> t p c", t=PACK)
+
+        nc.gpsimd.memset(wsraw[:].rearrange("p z c -> p (z c)").bitcast(I32), 0)
+        nc.gpsimd.memset(wbs[:].bitcast(I32), 0)
+        nc.scalar.dma_start(out=fac[:], in_=fk.rearrange("(z p t) o -> p z (t o)", z=PASSES, t=PACK))
+        for q in range(4):
+            nc.scalar.dma_start(out=wsraw[32 * q : 32 * q + 4, :, :].bitcast(I32),
+                                in_=w_scales[:, 4 * q : 4 * q + 4, :].rearrange("z q c -> q z c").bitcast(I32))
+
+        nc.sync.dma_start(l1[:], offs)
+        for z in range(PASSES):
+            nc.sync.dma_start(out=x[z][0][:], in_=xv[z, 0])
+            nc.sync.dma_start(out=ctr[z][:], in_=owv[z])
+            nc.sync.dma_start(out=x[z][1][:], in_=xv[z, 1])
+            nc.sync.dma_start(out=wraw[z][:].bitcast(I32), in_=w_words[z].rearrange("p c t -> p (c t)").bitcast(I32))
+            nc.sync.dma_start(out=x[z][2][:], in_=xv[z, 2])
+            nc.sync.dma_start(out=x[z][3][:], in_=xv[z, 3])
+        nc.sync.dma_start(l2[:], offs2)
+        nc.sync.dma_start(l3[:], offs3)
+        for t in (1, 0, 2, 3):
+            nc.sync.dma_start(out=old[t][:], in_=oldv[t])
+        nc.sync.dma_start(out=wb[:].bitcast(I32), in_=wb_words[0].bitcast(I32))
+        for q in range(4):
+            nc.sync.dma_start(out=wbs[32 * q : 32 * q + 4, :].bitcast(I32),
+                                in_=wb_scales[0, 4 * q : 4 * q + 4, :].bitcast(I32))
+        nc.sync.dma_start(out=bias[:], in_=bi[0, :].partition_broadcast(P))
+
+        for t in range(PACK):
+            nc.vector.memset(placed[t][:], 0.0)
+
+        acc = [psum.tile([P, J], F32, name="acc%d" % t) for t in range(PACK)]
+        for z in range(PASSES):
+            ub = keep.tile([P, J, PACK], BF16, name="ub%d" % z, align_bytes=64)
+            uq = keep.tile([P, J], U32, name="uq%d" % z, align_bytes=64)
+            us = keep.tile([P, J], U8, name="us%d" % z, align_bytes=64)
+            for t in range(PACK):
+                d = keep.tile([P, J], F32, name="d%d%d" % (z, t))
+                nc.vector.tensor_tensor(d[:], x[z][t][:].indirect(l1[:]), ctr[z][:, t, :], ALU.subtract)
+                if z == PASSES - 1 and t >= 2:
+                    nc.vector.tensor_scalar(ub[:, :, t], d[:], fac[:, z, t : t + 1], None, ALU.mult)
+                else:
+                    nc.scalar.activation(ub[:, :, t], d[:], ACT.Copy, scale=fac[:, z, t : t + 1])
+                if t == 1:
+                    nc.vector.tensor_copy(out=wd[z][:].rearrange("p (t m) -> p m t", t=PACK),
+                                          in_=wraw[z][:].rearrange("p (m t) -> p m t", t=PACK))
+                    if z == 0:
+                        nc.vector.tensor_copy(out=wsd[:].rearrange("p z (t m) -> p z t m", t=PACK),
+                                              in_=wsraw[:].rearrange("p z (m t) -> p z t m", t=PACK))
+            nc.vector.quantize_mx(out=uq[:].bitcast(E5M2), scales=us[:], in_=ub[:].rearrange("p j t -> p (j t)"))
+            for t in (1, 0, 2, 3):
+                cols = slice(P * t, P * (t + 1))
+                nc.tensor.matmul_mx(out=acc[t][:], lhsT=wd[z][:, cols].bitcast(E5M2), lhsT_scale=wsd[:, z, cols],
+                                    rhs=uq[:].bitcast(E5M2), rhs_scale=us[:], start=(z == 0), stop=(z == PASSES - 1))
+
+        ha = [keep.tile([P, J], F32, name="ha%d" % t) for t in range(PACK)]
+        nc.scalar.activation(ha[1][:], acc[1][:], ACT.Relu)
+        for t in (0, 2, 3):
+            nc.vector.tensor_scalar(ha[t][:], acc[t][:], 0.0, None, ALU.max)
+        nc.vector.tensor_copy(placed[0][:].indirect(l2[:]), ha[0][:])
+        for t in (1, 2, 3):
+            nc.scalar.activation(placed[t][:].indirect(l2[:]), ha[t][:], ACT.Copy)
+        for t in (1, 0, 2, 3):
+            nc.vector.tensor_tensor(page[t][:], placed[t][:], old[t][:], ALU.add)
+        g = keep.tile([P, PACK, O], BF16, name="g")
+        for t in (1, 0, 2):
+            nc.scalar.activation(g[:, t, :], page[t][:].indirect(l3[:]), ACT.Copy)
+        nc.vector.tensor_copy(g[:, 3, 0:HALF], page[3][:].indirect(l3[:, 0 : HALF // 16]))
+        nc.scalar.activation(g[:, 3, HALF:O], page[3][:].indirect(l3[:, HALF // 16 : O // 16]), ACT.Copy)
+
+        hb = [keep.tile([P, HALF, PACK], BF16, name="hb%d" % h, align_bytes=64) for h in range(2)]
+        hq = [keep.tile([P, HALF], U32, name="hq%d" % h, align_bytes=64) for h in range(2)]
+        hs = [keep.tile([P, HALF], U8, name="hs%d" % h, align_bytes=64) for h in range(2)]
+        pp = [psum.tile([P, N], F32, name="pp%d" % h) for h in range(2)]
+        for h in range(2):
+            nc.vector.tensor_copy(out=hb[h][:].rearrange("p (c i) t -> p c t i", i=4),
+                                  in_=g[:, :, HALF * h : HALF * (h + 1)].rearrange("p t (c i) -> p c t i", i=4))
+        for h in range(2):
+            nc.vector.quantize_mx(out=hq[h][:].bitcast(E5M2), scales=hs[h][:], in_=hb[h][:].rearrange("p o t -> p (o t)"))
+            nc.tensor.matmul_mx(out=pp[h][:], lhsT=hq[h][:].bitcast(E5M2), lhsT_scale=hs[h][:],
+                                rhs=wb[:].bitcast(E2M1), rhs_scale=wbs[:], start=True, stop=True)
+
+        nz = [keep.tile([P, N], F32, name="nz%d" % h) for h in range(2)]
+        low = [keep.tile([P, 1], F32, name="low%d" % h) for h in range(2)]
+        ea = [keep.tile([P, N], F32, name="ea%d" % h) for h in range(2)]
+        tot = [keep.tile([P, 1], F32, name="tot%d" % h) for h in range(2)]
+        rec = [keep.tile([P, 1], F32, name="rec%d" % h) for h in range(2)]
+        y = [keep.tile([P, N], F32, name="y%d" % h) for h in range(2)]
+        for h in range(2):
+            nc.vector.scalar_tensor_tensor(nz[h][:], pp[h][:], -0.7, bias[:], ALU.mult, ALU.subtract)
+        for h in range(2):
+            nc.vector.tensor_reduce(low[h][:], nz[h][:], AX.X, ALU.min)
+            nc.scalar.activation(ea[h][:], nz[h][:], ACT.Exp, bias=low[h][:], scale=-1.0, accum_out=tot[h][:])
+        for h in range(2):
+            nc.vector.reciprocal(rec[h][:], tot[h][:])
+            nc.vector.tensor_scalar(y[h][:], ea[h][:], rec[h][:], 256.0, ALU.mult, ALU.mult)
+            nc.sync.dma_start(out=out[HALF * h : HALF * (h + 1), :], in_=y[h][:])

@@ -21,6 +21,7 @@ P = 128
 PACK = 4
 PASSES = K // (P * PACK)
 HALF = O // 2
+HJ = J // 2
 
 
 def tile_list_page_offsetpicks_rowshares_kernel(tc, xf, ow, fk, w_words, w_scales, oldh, wb_words, wb_scales, bi, offs, offs2, offs3, out):
@@ -37,7 +38,6 @@ def tile_list_page_offsetpicks_rowshares_kernel(tc, xf, ow, fk, w_words, w_scale
         fac = keep.tile([P, PASSES, PACK], F32, name="fac")
         wraw = [keep.tile([P, R], U32, name="wraw%d" % z, align_bytes=64) for z in range(PASSES)]
         wsraw = keep.tile([P, PASSES, R], U8, name="wsraw", align_bytes=64)
-        wd = [keep.tile([P, R], U32, name="wd%d" % z, align_bytes=64) for z in range(PASSES)]
         wsd = keep.tile([P, PASSES, R], U8, name="wsd", align_bytes=64)
         old = [keep.tile([P, C], F32, name="old%d" % t) for t in range(PACK)]
         placed = [keep.tile([P, C], F32, name="placed%d" % t) for t in range(PACK)]
@@ -62,12 +62,12 @@ def tile_list_page_offsetpicks_rowshares_kernel(tc, xf, ow, fk, w_words, w_scale
             nc.sync.dma_start(out=x[z][0][:], in_=xv[z, 0])
             nc.sync.dma_start(out=ctr[z][:], in_=owv[z])
             nc.sync.dma_start(out=x[z][1][:], in_=xv[z, 1])
-            nc.sync.dma_start(out=wraw[z][:].bitcast(I32), in_=w_words[z].rearrange("p c t -> p (c t)").bitcast(I32))
             nc.sync.dma_start(out=x[z][2][:], in_=xv[z, 2])
             nc.sync.dma_start(out=x[z][3][:], in_=xv[z, 3])
+            nc.sync.dma_start(out=wraw[z][:].bitcast(I32), in_=w_words[z].rearrange("p c t -> p (c t)").bitcast(I32))
         nc.sync.dma_start(l2[:], offs2)
         nc.sync.dma_start(l3[:], offs3)
-        for t in (1, 0, 2, 3):
+        for t in range(PACK):
             nc.sync.dma_start(out=old[t][:], in_=oldv[t])
         nc.sync.dma_start(out=wb[:].bitcast(I32), in_=wb_words[0].bitcast(I32))
         for q in range(4):
@@ -76,7 +76,7 @@ def tile_list_page_offsetpicks_rowshares_kernel(tc, xf, ow, fk, w_words, w_scale
         nc.sync.dma_start(out=bias[:], in_=bi[0, :].partition_broadcast(P))
 
         for t in range(PACK):
-            nc.vector.memset(placed[t][:], 0.0)
+            nc.gpsimd.memset(placed[t][:], 0.0)
 
         acc = [psum.tile([P, J], F32, name="acc%d" % t) for t in range(PACK)]
         for z in range(PASSES):
@@ -84,38 +84,49 @@ def tile_list_page_offsetpicks_rowshares_kernel(tc, xf, ow, fk, w_words, w_scale
             uq = keep.tile([P, J], U32, name="uq%d" % z, align_bytes=64)
             us = keep.tile([P, J], U8, name="us%d" % z, align_bytes=64)
             for t in range(PACK):
-                d = keep.tile([P, J], F32, name="d%d%d" % (z, t))
-                nc.vector.tensor_tensor(d[:], x[z][t][:].indirect(l1[:]), ctr[z][:, t, :], ALU.subtract)
+                f = fac[:, z, t : t + 1]
                 if z == PASSES - 1 and t >= 2:
-                    nc.vector.tensor_scalar(ub[:, :, t], d[:], fac[:, z, t : t + 1], None, ALU.mult)
+                    dh = [keep.tile([P, HJ], F32, name="dh%d%d" % (t, h)) for h in range(2)]
+                    for h in range(2):
+                        nc.vector.tensor_tensor(dh[h][:], x[z][t][:].indirect(l1[:, h * HJ // 16 : (h + 1) * HJ // 16]),
+                                                ctr[z][:, t, h * HJ : (h + 1) * HJ], ALU.subtract)
+                    nc.scalar.activation(ub[:, 0:HJ, t], dh[0][:], ACT.Copy, scale=f)
+                    nc.vector.tensor_scalar(ub[:, HJ:J, t], dh[1][:], f, None, ALU.mult)
                 else:
-                    nc.scalar.activation(ub[:, :, t], d[:], ACT.Copy, scale=fac[:, z, t : t + 1])
-                if t == 1:
-                    nc.vector.tensor_copy(out=wd[z][:].rearrange("p (t m) -> p m t", t=PACK),
-                                          in_=wraw[z][:].rearrange("p (m t) -> p m t", t=PACK))
-                    if z == 0:
-                        nc.vector.tensor_copy(out=wsd[:].rearrange("p z (t m) -> p z t m", t=PACK),
-                                              in_=wsraw[:].rearrange("p z (m t) -> p z t m", t=PACK))
+                    d = keep.tile([P, J], F32, name="d%d%d" % (z, t))
+                    nc.vector.tensor_tensor(d[:], x[z][t][:].indirect(l1[:]), ctr[z][:, t, :], ALU.subtract)
+                    nc.scalar.activation(ub[:, :, t], d[:], ACT.Copy, scale=f)
+                if z == 0 and t == 0:
+                    nc.vector.tensor_copy(out=wsd[:].rearrange("p z (t m) -> p z t m", t=PACK),
+                                          in_=wsraw[:].rearrange("p z (m t) -> p z t m", t=PACK))
+            wsrc = wraw[z][:].rearrange("p (m t) -> p m t", t=PACK)
+            wd = keep.tile([P, PACK, P], U32, name="wd%d" % z, align_bytes=64)
+            nc.vector.tensor_copy(out=wd[:].rearrange("p t m -> p m t"), in_=wsrc)
             nc.vector.quantize_mx(out=uq[:].bitcast(E5M2), scales=us[:], in_=ub[:].rearrange("p j t -> p (j t)"))
-            for t in (1, 0, 2, 3):
-                cols = slice(P * t, P * (t + 1))
-                nc.tensor.matmul_mx(out=acc[t][:], lhsT=wd[z][:, cols].bitcast(E5M2), lhsT_scale=wsd[:, z, cols],
+            for t in range(PACK):
+                nc.tensor.matmul_mx(out=acc[t][:], lhsT=wd[:, t, :].bitcast(E5M2), lhsT_scale=wsd[:, z, P * t : P * (t + 1)],
                                     rhs=uq[:].bitcast(E5M2), rhs_scale=us[:], start=(z == 0), stop=(z == PASSES - 1))
 
         ha = [keep.tile([P, J], F32, name="ha%d" % t) for t in range(PACK)]
-        nc.scalar.activation(ha[1][:], acc[1][:], ACT.Relu)
-        for t in (0, 2, 3):
+        nc.scalar.activation(ha[0][:], acc[0][:], ACT.Relu)
+        nc.scalar.activation(placed[0][:].indirect(l2[:]), ha[0][:], ACT.Copy)
+        for t in (1, 3):
             nc.vector.tensor_scalar(ha[t][:], acc[t][:], 0.0, None, ALU.max)
-        nc.vector.tensor_copy(placed[0][:].indirect(l2[:]), ha[0][:])
-        for t in (1, 2, 3):
+        nc.vector.tensor_copy(placed[1][:].indirect(l2[:]), ha[1][:])
+        nc.scalar.activation(ha[2][:], acc[2][:], ACT.Relu)
+        for t in (2, 3):
             nc.scalar.activation(placed[t][:].indirect(l2[:]), ha[t][:], ACT.Copy)
-        for t in (1, 0, 2, 3):
+        for t in range(PACK):
             nc.vector.tensor_tensor(page[t][:], placed[t][:], old[t][:], ALU.add)
-        g = keep.tile([P, PACK, O], BF16, name="g")
-        for t in (1, 0, 2):
-            nc.scalar.activation(g[:, t, :], page[t][:].indirect(l3[:]), ACT.Copy)
-        nc.vector.tensor_copy(g[:, 3, 0:HALF], page[3][:].indirect(l3[:, 0 : HALF // 16]))
-        nc.scalar.activation(g[:, 3, HALF:O], page[3][:].indirect(l3[:, HALF // 16 : O // 16]), ACT.Copy)
+        g = [keep.tile([P, PACK, HALF], BF16, name="g0"), keep.tile([P, PACK, HALF], BF16, name="g1")]
+        for h in range(2):
+            for t in range(PACK):
+                dst = g[h][:, t, :]
+                src = page[t][:].indirect(l3[:, h * HALF // 16 : (h + 1) * HALF // 16])
+                if h == 0 and t == PACK - 1:
+                    nc.vector.tensor_copy(dst, src)
+                else:
+                    nc.scalar.activation(dst, src, ACT.Copy)
 
         hb = [keep.tile([P, HALF, PACK], BF16, name="hb%d" % h, align_bytes=64) for h in range(2)]
         hq = [keep.tile([P, HALF], U32, name="hq%d" % h, align_bytes=64) for h in range(2)]
@@ -123,8 +134,7 @@ def tile_list_page_offsetpicks_rowshares_kernel(tc, xf, ow, fk, w_words, w_scale
         pp = [psum.tile([P, N], F32, name="pp%d" % h) for h in range(2)]
         for h in range(2):
             nc.vector.tensor_copy(out=hb[h][:].rearrange("p (c i) t -> p c t i", i=4),
-                                  in_=g[:, :, HALF * h : HALF * (h + 1)].rearrange("p t (c i) -> p c t i", i=4))
-        for h in range(2):
+                                  in_=g[h][:].rearrange("p t (c i) -> p c t i", i=4))
             nc.vector.quantize_mx(out=hq[h][:].bitcast(E5M2), scales=hs[h][:], in_=hb[h][:].rearrange("p o t -> p (o t)"))
             nc.tensor.matmul_mx(out=pp[h][:], lhsT=hq[h][:].bitcast(E5M2), lhsT_scale=hs[h][:],
                                 rhs=wb[:].bitcast(E2M1), rhs_scale=wbs[:], start=True, stop=True)
@@ -137,7 +147,6 @@ def tile_list_page_offsetpicks_rowshares_kernel(tc, xf, ow, fk, w_words, w_scale
         y = [keep.tile([P, N], F32, name="y%d" % h) for h in range(2)]
         for h in range(2):
             nc.vector.scalar_tensor_tensor(nz[h][:], pp[h][:], -0.7, bias[:], ALU.mult, ALU.subtract)
-        for h in range(2):
             nc.vector.tensor_reduce(low[h][:], nz[h][:], AX.X, ALU.min)
             nc.scalar.activation(ea[h][:], nz[h][:], ACT.Exp, bias=low[h][:], scale=-1.0, accum_out=tot[h][:])
         for h in range(2):

from contextlib import ExitStack

import concourse.mybir as mybir

K, T, J, R, C, O, N = 1024, 1024, 256, 512, 1024, 256, 256
FLOPS = 2 * K * R * J + 2 * R * O * N

F32 = mybir.dt.float32
BF16 = mybir.dt.bfloat16
I32 = mybir.dt.int32
U32 = mybir.dt.uint32
U16 = mybir.dt.uint16
U8 = mybir.dt.uint8
E5M2 = mybir.dt.float8_e5m2_x4
E2M1 = mybir.dt.float4_e2m1fn_x4
ALU = mybir.AluOpType
ACT = mybir.ActivationFunctionType
AX = mybir.AxisListType

P = 128
PACK = 4
PASSES = K // (P * PACK)
HALF = O // 2
HJ = J // 2


def tile_list_page_offsetpicks_rowshares_kernel(tc, xf, ow, fk, w_words, w_scales, oldh, wb_words, wb_scales, bi, offs, offs2, offs3, out):
    nc = tc.nc
    with ExitStack() as ctx:
        keep = ctx.enter_context(tc.tile_pool(name="keep", bufs=1))
        psum = ctx.enter_context(tc.psum_pool(name="psum", bufs=1))

        l1 = keep.tile([P, J // 16], U16, name="l1")
        l2 = keep.tile([P, J // 16], U16, name="l2")
        l3 = keep.tile([P, O // 16], U16, name="l3")
        x = [[keep.tile([P, T], F32, name="x%d%d" % (z, t)) for t in range(PACK)] for z in range(PASSES)]
        ctr = [keep.tile([P, PACK, J], F32, name="ctr%d" % z) for z in range(PASSES)]
        fac = keep.tile([P, PASSES, PACK], F32, name="fac")
        wraw = [keep.tile([P, R], U32, name="wraw%d" % z, align_bytes=64) for z in range(PASSES)]
        wsraw = keep.tile([P, PASSES, R], U8, name="wsraw", align_bytes=64)
        wsd = keep.tile([P, PASSES, R], U8, name="wsd", align_bytes=64)
        old = [keep.tile([P, C], F32, name="old%d" % t) for t in range(PACK)]
        placed = [keep.tile([P, C], F32, name="placed%d" % t) for t in range(PACK)]
        page = [keep.tile([P, C], F32, name="page%d" % t) for t in range(PACK)]
        wb = keep.tile([P, 2 * N], U8, name="wb", align_bytes=64)
        wbs = keep.tile([P, N], U8, name="wbs", align_bytes=64)
        bias = keep.tile([P, N], F32, name="bias")

        xv = xf.rearrange("(z p t) c -> z t p c", z=PASSES, t=PACK)
        owv = ow.rearrange("(z p t) j -> z p t j", z=PASSES, t=PACK)
        oldv = oldh.rearrange("(p t) c -> t p c", t=PACK)

        nc.gpsimd.memset(wsraw[:].rearrange("p z c -> p (z c)").bitcast(I32), 0)
        nc.gpsimd.memset(wbs[:].bitcast(I32), 0)
        nc.scalar.dma_start(out=fac[:], in_=fk.rearrange("(z p t) o -> p z (t o)", z=PASSES, t=PACK))
        for q in range(4):
            nc.scalar.dma_start(out=wsraw[32 * q : 32 * q + 4, :, :].bitcast(I32),
                                in_=w_scales[:, 4 * q : 4 * q + 4, :].rearrange("z q c -> q z c").bitcast(I32))

        nc.sync.dma_start(l1[:], offs)
        for z in range(PASSES):
            nc.sync.dma_start(out=x[z][0][:], in_=xv[z, 0])
            nc.sync.dma_start(out=ctr[z][:], in_=owv[z])
            nc.sync.dma_start(out=x[z][1][:], in_=xv[z, 1])
            nc.sync.dma_start(out=x[z][2][:], in_=xv[z, 2])
            nc.sync.dma_start(out=x[z][3][:], in_=xv[z, 3])
            nc.sync.dma_start(out=wraw[z][:].bitcast(I32), in_=w_words[z].rearrange("p c t -> p (c t)").bitcast(I32))
        nc.sync.dma_start(l2[:], offs2)
        nc.sync.dma_start(l3[:], offs3)
        for t in range(PACK):
            nc.sync.dma_start(out=old[t][:], in_=oldv[t])
        nc.sync.dma_start(out=wb[:].bitcast(I32), in_=wb_words[0].bitcast(I32))
        for q in range(4):
            nc.sync.dma_start(out=wbs[32 * q : 32 * q + 4, :].bitcast(I32),
                                in_=wb_scales[0, 4 * q : 4 * q + 4, :].bitcast(I32))
        nc.sync.dma_start(out=bias[:], in_=bi[0, :].partition_broadcast(P))

        for t in range(PACK):
            nc.gpsimd.memset(placed[t][:], 0.0)

        acc = [psum.tile([P, J], F32, name="acc%d" % t) for t in range(PACK)]
        for z in range(PASSES):
            ub = keep.tile([P, J, PACK], BF16, name="ub%d" % z, align_bytes=64)
            uq = keep.tile([P, J], U32, name="uq%d" % z, align_bytes=64)
            us = keep.tile([P, J], U8, name="us%d" % z, align_bytes=64)
            for t in range(PACK):
                f = fac[:, z, t : t + 1]
                if z == PASSES - 1 and t >= 2:
                    dh = [keep.tile([P, HJ], F32, name="dh%d%d" % (t, h)) for h in range(2)]
                    for h in range(2):
                        nc.vector.tensor_tensor(dh[h][:], x[z][t][:].indirect(l1[:, h * HJ // 16 : (h + 1) * HJ // 16]),
                                                ctr[z][:, t, h * HJ : (h + 1) * HJ], ALU.subtract)
                    nc.scalar.activation(ub[:, 0:HJ, t], dh[0][:], ACT.Copy, scale=f)
                    nc.vector.tensor_scalar(ub[:, HJ:J, t], dh[1][:], f, None, ALU.mult)
                else:
                    d = keep.tile([P, J], F32, name="d%d%d" % (z, t))
                    nc.vector.tensor_tensor(d[:], x[z][t][:].indirect(l1[:]), ctr[z][:, t, :], ALU.subtract)
                    nc.scalar.activation(ub[:, :, t], d[:], ACT.Copy, scale=f)
                if z == 0 and t == 0:
                    nc.vector.tensor_copy(out=wsd[:].rearrange("p z (t m) -> p z t m", t=PACK),
                                          in_=wsraw[:].rearrange("p z (m t) -> p z t m", t=PACK))
            wsrc = wraw[z][:].rearrange("p (m t) -> p m t", t=PACK)
            wd = keep.tile([P, PACK, P], U32, name="wd%d" % z, align_bytes=64)
            nc.vector.tensor_copy(out=wd[:].rearrange("p t m -> p m t"), in_=wsrc)
            nc.vector.quantize_mx(out=uq[:].bitcast(E5M2), scales=us[:], in_=ub[:].rearrange("p j t -> p (j t)"))
            for t in range(PACK):
                nc.tensor.matmul_mx(out=acc[t][:], lhsT=wd[:, t, :].bitcast(E5M2), lhsT_scale=wsd[:, z, P * t : P * (t + 1)],
                                    rhs=uq[:].bitcast(E5M2), rhs_scale=us[:], start=(z == 0), stop=(z == PASSES - 1))

        ha = [keep.tile([P, J], F32, name="ha%d" % t) for t in range(PACK)]
        nc.scalar.activation(ha[0][:], acc[0][:], ACT.Relu)
        nc.scalar.activation(placed[0][:].indirect(l2[:]), ha[0][:], ACT.Copy)
        for t in (1, 3):
            nc.vector.tensor_scalar(ha[t][:], acc[t][:], 0.0, None, ALU.max)
        nc.vector.tensor_copy(placed[1][:].indirect(l2[:]), ha[1][:])
        nc.scalar.activation(ha[2][:], acc[2][:], ACT.Relu)
        for t in (2, 3):
            nc.scalar.activation(placed[t][:].indirect(l2[:]), ha[t][:], ACT.Copy)
        for t in range(PACK):
            nc.vector.tensor_tensor(page[t][:], placed[t][:], old[t][:], ALU.add)
        g = [keep.tile([P, PACK, HALF], BF16, name="g0"), keep.tile([P, PACK, HALF], BF16, name="g1")]
        for h in range(2):
            for t in range(PACK):
                dst = g[h][:, t, :]
                src = page[t][:].indirect(l3[:, h * HALF // 16 : (h + 1) * HALF // 16])
                if h == 0 and t == PACK - 1:
                    nc.vector.tensor_copy(dst, src)
                else:
                    nc.scalar.activation(dst, src, ACT.Copy)

        hb = [keep.tile([P, HALF, PACK], BF16, name="hb%d" % h, align_bytes=64) for h in range(2)]
        hq = [keep.tile([P, HALF], U32, name="hq%d" % h, align_bytes=64) for h in range(2)]
        hs = [keep.tile([P, HALF], U8, name="hs%d" % h, align_bytes=64) for h in range(2)]
        pp = [psum.tile([P, N], F32, name="pp%d" % h) for h in range(2)]
        for h in range(2):
            nc.vector.tensor_copy(out=hb[h][:].rearrange("p (c i) t -> p c t i", i=4),
                                  in_=g[h][:].rearrange("p t (c i) -> p c t i", i=4))
            nc.vector.quantize_mx(out=hq[h][:].bitcast(E5M2), scales=hs[h][:], in_=hb[h][:].rearrange("p o t -> p (o t)"))
            nc.tensor.matmul_mx(out=pp[h][:], lhsT=hq[h][:].bitcast(E5M2), lhsT_scale=hs[h][:],
                                rhs=wb[:].bitcast(E2M1), rhs_scale=wbs[:], start=True, stop=True)

        nz = [keep.tile([P, N], F32, name="nz%d" % h) for h in range(2)]
        low = [keep.tile([P, 1], F32, name="low%d" % h) for h in range(2)]
        ea = [keep.tile([P, N], F32, name="ea%d" % h) for h in range(2)]
        tot = [keep.tile([P, 1], F32, name="tot%d" % h) for h in range(2)]
        rec = [keep.tile([P, 1], F32, name="rec%d" % h) for h in range(2)]
        y = [keep.tile([P, N], F32, name="y%d" % h) for h in range(2)]
        for h in range(2):
            nc.vector.scalar_tensor_tensor(nz[h][:], pp[h][:], -0.7, bias[:], ALU.mult, ALU.subtract)
            nc.vector.tensor_reduce(low[h][:], nz[h][:], AX.X, ALU.min)
            nc.scalar.activation(ea[h][:], nz[h][:], ACT.Exp, bias=low[h][:], scale=-1.0, accum_out=tot[h][:])
        for h in range(2):
            nc.vector.reciprocal(rec[h][:], tot[h][:])
            nc.vector.tensor_scalar(y[h][:], ea[h][:], rec[h][:], 256.0, ALU.mult, ALU.mult)
            nc.sync.dma_start(out=out[HALF * h : HALF * (h + 1), :], in_=y[h][:])
